import numpy as np
import ml_dtypes


def mxq(x, axis, fmt="e4m3"):
    dtype, down = {"e4m3": (ml_dtypes.float8_e4m3fn, 7), "e5m2": (ml_dtypes.float8_e5m2, 14)}[fmt]
    v = np.moveaxis(np.asarray(x, np.float32).astype(ml_dtypes.bfloat16).astype(np.float64), axis, -1)
    blocks = v.reshape(v.shape[:-1] + (-1, 32))
    amax = np.abs(blocks).max(-1, keepdims=True)
    byte = np.maximum(np.where(amax > 0, np.frexp(amax)[1] - 1 + 127, 0) - down, 1)
    scale = np.exp2(byte - 127.0)
    codes = (blocks / scale).astype(np.float32).astype(dtype).astype(np.float64)
    return np.moveaxis((codes * scale).reshape(v.shape), -1, axis)


WIDE = False


def mx_kscale(k):
    if not WIDE:
        return np.ones(k)
    levels = np.array([10, -10, 5, -5, 0])
    if k % 512:
        return np.exp2(np.random.permutation(np.resize(levels, k // 32))).repeat(32)
    a = np.empty((k // 512, 16))
    for p in range(k // 512):
        a[p, :8] = np.random.permutation(np.resize(levels, 8))
        for g in range(8):
            far = levels[np.abs(levels - a[p, g]) >= 10]
            a[p, g + 8] = far[np.random.randint(len(far))]
    return np.exp2(a.ravel()).repeat(32)


def f64(x):
    return np.asarray(x).astype(np.float64)


def striped(idx):
    return np.tile(idx.reshape(-1, 16).T, (8, 1)).astype(np.uint16)


def unstriped(offs):
    return offs[:16].T.reshape(-1).astype(np.int64)


E2M1 = np.array([0.0, 0.5, 1.0, 1.5, 2.0, 3.0, 4.0, 6.0, -0.0, -0.5, -1.0, -1.5, -2.0, -3.0, -4.0, -6.0])


def pack_weight(w, fmt):
    k, n = w.shape
    w = f64(np.asarray(w, np.float32).astype(ml_dtypes.bfloat16)).reshape(k // 32, 32, n)
    amax = np.abs(w).max(1)
    if fmt == "e4m3":
        byte = np.frexp(amax)[1] - 1 + 127 - 7
    else:
        mant, ex = np.frexp(amax / 6.0)
        byte = np.where(mant > 0.5, ex, ex - 1) + 127
    byte = np.clip(np.where(amax > 0, byte, 1), 1, 254)
    scaled = (w * np.exp2(127.0 - byte)[:, None, :]).reshape(k, n).astype(np.float32)
    by_word = np.ascontiguousarray(scaled.reshape(k // 512, 128, 4, n).transpose(0, 1, 3, 2))
    if fmt == "e4m3":
        words = by_word.astype(ml_dtypes.float8_e4m3fn).view(np.uint8)
    else:
        c = by_word.astype(ml_dtypes.float4_e2m1fn).view(np.uint8) & 0xF
        words = (c[..., 0::2] | (c[..., 1::2] << 4)).reshape(k // 512, 128, 2 * n)
    return np.ascontiguousarray(words), np.ascontiguousarray(byte.astype(np.uint8).reshape(k // 512, 16, n))


def unpack_weight(words, scales, fmt):
    g, _, n = scales.shape
    words = np.ascontiguousarray(words).reshape(g, 128, n, -1)
    if fmt == "e4m3":
        vals = words.view(ml_dtypes.float8_e4m3fn).astype(np.float64)
    else:
        nib = np.empty((g, 128, n, 4), np.uint8)
        nib[..., 0::2] = words & 0xF
        nib[..., 1::2] = words >> 4
        vals = E2M1[nib]
    vals = vals * np.repeat(np.exp2(scales.astype(np.float64) - 127.0), 8, axis=1)[..., None]
    return vals.transpose(0, 1, 3, 2).reshape(g * 512, n)


def silu(v):
    return v / (1.0 + np.exp(-np.maximum(v, -700.0)))


K, T, E, C, N = 2048, 768, 8, 128, 256
PAD = 32
K8 = 1024


def by_expert(wq, xq):
    return np.concatenate([wq[e].T @ xq[:, e * C:(e + 1) * C] for e in range(E)], axis=1)


def setup_inputs():
    n = np.random.standard_normal
    s = mx_kscale(K)[:, None]
    first = np.random.permutation(np.repeat(np.arange(E), T // E))
    second = (first + 1 + np.random.permutation(np.repeat(np.arange(E - 1), -(-T // (E - 1)))[:T])) % E
    while np.bincount(second, minlength=E).max() != T // E:
        load = np.bincount(second, minlength=E); hi, lo = int(load.argmax()), int(load.argmin())
        t = np.flatnonzero((second == hi) & (first != lo))[0]; second[t] = lo
    slot_token = np.empty(E * C, np.int64); pos = np.empty((2, T), np.int64); fill = np.zeros(E, np.int64)
    place = np.stack([np.random.permutation(C) for _ in range(E)])
    for r, deal in enumerate((first, second)):
        for t in np.random.permutation(T):
            e = deal[t]
            if fill[e] < C: j = e * C + place[e, fill[e]]; fill[e] += 1; slot_token[j] = t; pos[r, t] = j
            else: pos[r, t] = E * C + t % PAD
    g = np.random.uniform(0.2, 0.8, T)
    w = n((E, K, N)) / np.sqrt(K) / s[None]
    w8 = [pack_weight(m[:K8], "e4m3") for m in w]
    w4 = [pack_weight(m[K8:], "e2m1") for m in w]
    return {
        "xT": (n((K, T)) * s).astype(np.float32),
        "w8_words": np.stack([m[0] for m in w8]),
        "w8_scales": np.stack([m[1] for m in w8]),
        "w4_words": np.stack([m[0] for m in w4]),
        "w4_scales": np.stack([m[1] for m in w4]),
        "b": (0.3 * n((N, E))).astype(np.float32),
        "gate": np.stack([np.tile(g, (N, 1)), np.tile(1.0 - g, (N, 1))]).astype(np.float32),
        "offs": striped(slot_token),
        "pos1": striped(pos[0]),
        "pos2": striped(pos[1]),
    }


def reference(xT, w8_words, w8_scales, w4_words, w4_scales, b, gate, offs, pos1, pos2):
    idx = unstriped(offs)
    w = np.stack([np.concatenate([unpack_weight(w8_words[e], w8_scales[e], "e4m3"), unpack_weight(w4_words[e], w4_scales[e], "e2m1")]) for e in range(E)])
    xq = mxq(f64(xT)[:, idx], 0, "e4m3")
    y = by_expert(w, xq)
    y = silu(y + np.repeat(f64(b), C, axis=1))
    y = np.concatenate([y, np.zeros((N, PAD))], axis=1)
    return f64(gate[0]) * y[:, unstriped(pos1)] + f64(gate[1]) * y[:, unstriped(pos2)]

@@ -1,0 +1,171 @@
+from contextlib import ExitStack
+
+import concourse.mybir as mybir
+
+K, T, E, C, N = 2048, 768, 8, 128, 256
+S = E * C
+PAD = 32
+P = 128
+PACK = 4
+FLOPS = 2 * K * S * N
+BYTES = 4 * K * T + 3 * E * K * N // 4 + 2 * E * K * N // 64 + 4 * N * E + 4 * 2 * P * T + 2 * P * (S + 2 * T) // 16 + 4 * N * T
+
+F32 = mybir.dt.float32
+BF16 = mybir.dt.bfloat16
+U32 = mybir.dt.uint32
+I32 = mybir.dt.int32
+U16 = mybir.dt.uint16
+U8 = mybir.dt.uint8
+FP8X4 = mybir.dt.float8_e4m3fn_x4
+FP4X4 = mybir.dt.float4_e2m1fn_x4
+SILU = mybir.ActivationFunctionType.Silu
+MULT = mybir.AluOpType.mult
+ADD = mybir.AluOpType.add
+
+ORDER = ((0, 0, 4), (2, 0, 0), (1, 1, 4), (3, 1, 0))
+CHUNKS = {0: (256, 256, 256), 2: (512, 256), 1: (512, 256), 3: (256, 256, 256)}
+LOADS = {0: (256, 512), 2: (768,), 1: (768,), 3: (768,)}
+ON_VECTOR = ((0, 1), (3, 1))
+
+
+def tile_moe_cap2_lin_silu_kernel(
+    tc, xT, w8_words, w8_scales, w4_words, w4_scales, b, gate, offs, pos1, pos2, out
+):
+    nc = tc.nc
+    with ExitStack() as ctx:
+        lists = ctx.enter_context(tc.tile_pool(name="lists", bufs=1))
+        keep = ctx.enter_context(tc.tile_pool(name="keep", bufs=1))
+        psum = ctx.enter_context(tc.psum_pool(name="psum", bufs=8))
+
+        offs_t = lists.tile([P, S // 16], U16, name="offs_t")
+        pos1_t = lists.tile([P, T // 16], U16, name="pos1_t")
+        pos2_t = lists.tile([P, T // 16], U16, name="pos2_t")
+
+        w4_t = keep.tile([P, 2 * E, 2 * N], U8, name="w4_t", align_bytes=64)
+        w8_t = [keep.tile([P, 2 * E, 4 * P], U8, name=f"w8_t{h}", align_bytes=64) for h in range(2)]
+        w8s_t = keep.tile([P, 2 * E, N], U8, name="w8s_t", align_bytes=64)
+        w4s_t = keep.tile([P, 2 * E, N], U8, name="w4s_t", align_bytes=64)
+        bias_t = keep.tile([P, 2, E], F32, name="bias_t")
+        gate_t = [keep.tile([P, T], F32, name=f"gate_t{i}") for i in range(2)]
+        y_t = [keep.tile([P, S + PAD], F32, name=f"y_t{h}") for h in range(2)]
+        planes = [keep.tile([P, T], U8, name=f"planes{i}", align_bytes=64) for i in range(2)]
+        gplanes = [keep.tile([P, S], U8, name=f"gplanes{i}", align_bytes=64) for i in range(2)]
+        codes = [keep.tile([P, T], U32, name=f"codes{g}", align_bytes=64) for g in range(4)]
+        gcodes = [keep.tile([P, S], U32, name=f"gcodes{g}", align_bytes=64) for g in range(4)]
+
+        warm = keep.tile([P, 8], F32, name="warm")
+        nc.vector.memset(warm[:], 0.0)
+        warm2 = keep.tile([P, 8], F32, name="warm2")
+        nc.scalar.activation(warm2[:], warm[:], SILU)
+
+        for i in range(2):
+            nc.gpsimd.memset(planes[i][:].bitcast(I32), 0)
+        for t in (w8s_t, w4s_t):
+            nc.vector.memset(t[:].rearrange("p a n -> p (a n)").bitcast(I32), 0)
+        for h in range(2):
+            nc.gpsimd.memset(y_t[h][:, S : S + PAD], 0.0)
+
+        nc.sync.dma_start(offs_t[:], offs)
+        raw = {}
+        for g, _, _ in ORDER:
+            rows = xT[512 * g : 512 * (g + 1), :].rearrange("(p j) w -> p j w", j=PACK)
+            c0 = 0
+            for w in LOADS[g]:
+                r = keep.tile([P, PACK, w], F32, name=f"raw{g}_{c0}")
+                nc.sync.dma_start(r[:], rows[:, :, c0 : c0 + w])
+                raw[g, c0] = r
+                c0 += w
+        nc.gpsimd.dma_start(bias_t[:], b.rearrange("(h p) e -> p h e", h=2))
+        for dram, t in ((w4_scales, w4s_t), (w8_scales, w8s_t)):
+            v = dram.rearrange("e a q n -> q (e a) n")
+            for q in range(4):
+                nc.sync.dma_start(
+                    t[32 * q : 32 * q + 4, :, :].bitcast(I32), v[4 * q : 4 * q + 4, :, :].bitcast(I32)
+                )
+        w4_v = w4_words.rearrange("e a p m -> p (e a) m")
+        for i in range(2):
+            s = slice(8 * i, 8 * i + 8)
+            nc.sync.dma_start(w4_t[:, s, :].bitcast(I32), w4_v[:, s, :].bitcast(I32))
+        w8_v = w8_words.rearrange("e a p n r -> p (e a) (n r)")
+
+        def load_w8(h, parts):
+            n = 16 // parts
+            for i in range(parts):
+                s = slice(n * i, n * i + n)
+                nc.sync.dma_start(
+                    w8_t[h][:, s, :].bitcast(I32), w8_v[:, s, 512 * h : 512 * h + 512].bitcast(I32)
+                )
+
+        load_w8(0, 4)
+        nc.sync.dma_start(pos1_t[:], pos1)
+        nc.sync.dma_start(gate_t[0][:], gate[0, 0:P, :])
+        nc.sync.dma_start(pos2_t[:], pos2)
+        nc.sync.dma_start(gate_t[1][:], gate[1, 0:P, :])
+        load_w8(1, 4)
+
+        def gather(dst, table, pieces):
+            n = S // pieces
+            for i in range(pieces):
+                nc.vector.tensor_copy(
+                    dst[:, n * i : n * i + n], table[:].indirect(offs_t[:, n * i // 16 : (n * i + n) // 16])
+                )
+
+        for k, (g, i, row) in enumerate(ORDER):
+            c0 = 0
+            for ci, w in enumerate(CHUNKS[g]):
+                base = max(c for (gg, c) in raw if gg == g and c <= c0)
+                src = raw[g, base][:, :, c0 - base : c0 - base + w].rearrange("p t (c i) -> p c t i", i=4)
+                grouped = keep.tile([P, w, PACK], BF16, name=f"grouped{g}_{c0}", align_bytes=64)
+                dst = grouped[:].rearrange("p (c i) t -> p c t i", i=4)
+                if (g, ci) in ON_VECTOR:
+                    nc.vector.tensor_copy(dst, src)
+                else:
+                    nc.scalar.copy(dst, src)
+                nc.vector.quantize_mx(
+                    out=codes[g][:, c0 : c0 + w].bitcast(FP8X4),
+                    scales=planes[i][row:P, c0 : c0 + w],
+                    in_=grouped[:].rearrange("p w t -> p (w t)"),
+                )
+                c0 += w
+            if k % 2 == 1:
+                gather(gplanes[i], planes[i], 2)
+            gather(gcodes[g], codes[g], 2)
+
+        for h in range(2):
+            banks = []
+            for e in range(E):
+                slots = slice(C * e, C * e + C)
+                acc = psum.tile([P, C], F32, name="acc")
+                banks.append(acc)
+                for a in range(2):
+                    nc.tensor.matmul_mx(
+                        out=acc[:],
+                        lhsT=w4_t[:, 2 * e + a, 2 * P * h : 2 * P * h + 2 * P].bitcast(FP4X4),
+                        lhsT_scale=w4s_t[:, 2 * e + a, P * h : P * h + P],
+                        rhs=gcodes[2 + a][:, slots].bitcast(FP8X4),
+                        rhs_scale=gplanes[a][:, slots],
+                        start=(a == 0),
+                        stop=False,
+                    )
+            for e in range(E):
+                slots = slice(C * e, C * e + C)
+                for a in range(2):
+                    nc.tensor.matmul_mx(
+                        out=banks[e][:],
+                        lhsT=w8_t[h][:, 2 * e + a, :].bitcast(FP8X4),
+                        lhsT_scale=w8s_t[:, 2 * e + a, P * h : P * h + P],
+                        rhs=gcodes[a][:, slots].bitcast(FP8X4),
+                        rhs_scale=gplanes[a][4:P, slots],
+                        start=False,
+                        stop=(a == 1),
+                    )
+                nc.scalar.activation(y_t[h][:, slots], banks[e][:], SILU, bias=bias_t[:, h, e : e + 1])
+
+        for h in range(2):
+            first = keep.tile([P, T], F32, name=f"first{h}")
+            second = keep.tile([P, T], F32, name=f"second{h}")
+            result = keep.tile([P, T], F32, name=f"result{h}")
+            nc.vector.tensor_tensor(first[:], y_t[h][:].indirect(pos1_t[:]), gate_t[0][:], MULT)
+            nc.vector.tensor_tensor(second[:], y_t[h][:].indirect(pos2_t[:]), gate_t[1][:], MULT)
+            nc.vector.tensor_tensor(result[:], first[:], second[:], ADD)
+            nc.sync.dma_start(out[P * h : P * h + P, :], result[:])

@@ -22,10 +22,10 @@ SILU = mybir.ActivationFunctionType.Silu
 MULT = mybir.AluOpType.mult
 ADD = mybir.AluOpType.add
 
-ORDER = ((0, 0, 4), (2, 0, 0), (1, 1, 4), (3, 1, 0))
-CHUNKS = {0: (256, 256, 256), 2: (512, 256), 1: (512, 256), 3: (256, 256, 256)}
-LOADS = {0: (256, 512), 2: (768,), 1: (768,), 3: (768,)}
-ON_VECTOR = ((0, 1), (3, 1))
+ORDER = ((0, 4), (2, 0), (1, 8), (3, 12))
+CHUNKS = {0: (256, 256, 256), 2: (512, 256), 1: (512, 256), 3: (512, 256)}
+LOADS = {0: (512, 256), 2: (512, 256), 1: (512, 256), 3: (512, 256)}
+ON_VECTOR = ((0, 1), (0, 2), (2, 1))
 
 
 def tile_moe_cap2_lin_silu_kernel(
@@ -46,10 +46,11 @@ def tile_moe_cap2_lin_silu_kernel(
         w8s_t = keep.tile([P, 2 * E, N], U8, name="w8s_t", align_bytes=64)
         w4s_t = keep.tile([P, 2 * E, N], U8, name="w4s_t", align_bytes=64)
         bias_t = keep.tile([P, 2, E], F32, name="bias_t")
-        gate_t = [keep.tile([P, T], F32, name=f"gate_t{i}") for i in range(2)]
+        gate_t = keep.tile([P, 2, T], F32, name="gate_t")
         y_t = [keep.tile([P, S + PAD], F32, name=f"y_t{h}") for h in range(2)]
-        planes = [keep.tile([P, T], U8, name=f"planes{i}", align_bytes=64) for i in range(2)]
-        gplanes = [keep.tile([P, S], U8, name=f"gplanes{i}", align_bytes=64) for i in range(2)]
+        planes = keep.tile([P, T], U8, name="planes", align_bytes=64)
+        gplanes = keep.tile([P, S], U8, name="gplanes", align_bytes=64)
+        moved = keep.tile([P, S], U8, name="moved", align_bytes=64)
         codes = [keep.tile([P, T], U32, name=f"codes{g}", align_bytes=64) for g in range(4)]
         gcodes = [keep.tile([P, S], U32, name=f"gcodes{g}", align_bytes=64) for g in range(4)]
 
@@ -58,16 +59,16 @@ def tile_moe_cap2_lin_silu_kernel(
         warm2 = keep.tile([P, 8], F32, name="warm2")
         nc.scalar.activation(warm2[:], warm[:], SILU)
 
-        for i in range(2):
-            nc.gpsimd.memset(planes[i][:].bitcast(I32), 0)
+        nc.gpsimd.memset(planes[:].bitcast(I32), 0)
+        nc.gpsimd.memset(moved[:].bitcast(I32), 0)
         for t in (w8s_t, w4s_t):
             nc.vector.memset(t[:].rearrange("p a n -> p (a n)").bitcast(I32), 0)
         for h in range(2):
-            nc.gpsimd.memset(y_t[h][:, S : S + PAD], 0.0)
+            nc.vector.memset(y_t[h][:, S : S + PAD], 0.0)
 
         nc.sync.dma_start(offs_t[:], offs)
         raw = {}
-        for g, _, _ in ORDER:
+        for g, _ in ORDER:
             rows = xT[512 * g : 512 * (g + 1), :].rearrange("(p j) w -> p j w", j=PACK)
             c0 = 0
             for w in LOADS[g]:
@@ -79,13 +80,11 @@ def tile_moe_cap2_lin_silu_kernel(
         for dram, t in ((w4_scales, w4s_t), (w8_scales, w8s_t)):
             v = dram.rearrange("e a q n -> q (e a) n")
             for q in range(4):
-                nc.sync.dma_start(
+                nc.gpsimd.dma_start(
                     t[32 * q : 32 * q + 4, :, :].bitcast(I32), v[4 * q : 4 * q + 4, :, :].bitcast(I32)
                 )
         w4_v = w4_words.rearrange("e a p m -> p (e a) m")
-        for i in range(2):
-            s = slice(8 * i, 8 * i + 8)
-            nc.sync.dma_start(w4_t[:, s, :].bitcast(I32), w4_v[:, s, :].bitcast(I32))
+        nc.sync.dma_start(w4_t[:].bitcast(I32), w4_v.bitcast(I32))
         w8_v = w8_words.rearrange("e a p n r -> p (e a) (n r)")
 
         def load_w8(h, parts):
@@ -96,21 +95,19 @@ def tile_moe_cap2_lin_silu_kernel(
                     w8_t[h][:, s, :].bitcast(I32), w8_v[:, s, 512 * h : 512 * h + 512].bitcast(I32)
                 )
 
-        load_w8(0, 4)
+        load_w8(0, 2)
         nc.sync.dma_start(pos1_t[:], pos1)
-        nc.sync.dma_start(gate_t[0][:], gate[0, 0:P, :])
         nc.sync.dma_start(pos2_t[:], pos2)
-        nc.sync.dma_start(gate_t[1][:], gate[1, 0:P, :])
-        load_w8(1, 4)
+        nc.sync.dma_start(gate_t[:], gate[:, 0:P, :].rearrange("i p t -> p i t"))
+        load_w8(1, 2)
 
         def gather(dst, table, pieces):
-            n = S // pieces
-            for i in range(pieces):
-                nc.vector.tensor_copy(
-                    dst[:, n * i : n * i + n], table[:].indirect(offs_t[:, n * i // 16 : (n * i + n) // 16])
-                )
+            j = 0
+            for n in pieces:
+                nc.vector.tensor_copy(dst[:, j : j + n], table[:].indirect(offs_t[:, j // 16 : (j + n) // 16]))
+                j += n
 
-        for k, (g, i, row) in enumerate(ORDER):
+        for k, (g, row) in enumerate(ORDER):
             c0 = 0
             for ci, w in enumerate(CHUNKS[g]):
                 base = max(c for (gg, c) in raw if gg == g and c <= c0)
@@ -123,49 +120,73 @@ def tile_moe_cap2_lin_silu_kernel(
                     nc.scalar.copy(dst, src)
                 nc.vector.quantize_mx(
                     out=codes[g][:, c0 : c0 + w].bitcast(FP8X4),
-                    scales=planes[i][row:P, c0 : c0 + w],
+                    scales=planes[row:P, c0 : c0 + w],
                     in_=grouped[:].rearrange("p w t -> p (w t)"),
                 )
                 c0 += w
-            if k % 2 == 1:
-                gather(gplanes[i], planes[i], 2)
-            gather(gcodes[g], codes[g], 2)
+            if k == 3:
+                gather(gplanes, planes, (512, 512))
+                for q in range(0, P, 32):
+                    nc.scalar.dma_start(
+                        moved[q : q + 4, :].bitcast(I32), gplanes[q + row : q + row + 4, :].bitcast(I32)
+                    )
+            gather(gcodes[g], codes[g], (512, 384, 128) if k == 3 else (512, 512))
+
+        def multiply(acc, h, e, g, start, stop):
+            slots = slice(C * e, C * e + C)
+            a = g % 2
+            if g < 2:
+                w, ws = w8_t[h][:, 2 * e + a, :].bitcast(FP8X4), w8s_t
+            else:
+                w, ws = w4_t[:, 2 * e + a, 2 * P * h : 2 * P * h + 2 * P].bitcast(FP4X4), w4s_t
+            plane = moved if g == 3 else gplanes
+            row = 0 if g == 3 else dict(ORDER)[g]
+            nc.tensor.matmul_mx(
+                out=acc[:],
+                lhsT=w,
+                lhsT_scale=ws[:, 2 * e + a, P * h : P * h + P],
+                rhs=gcodes[g][:, slots].bitcast(FP8X4),
+                rhs_scale=plane[row:P, slots],
+                start=start,
+                stop=stop,
+            )
 
         for h in range(2):
             banks = []
             for e in range(E):
-                slots = slice(C * e, C * e + C)
                 acc = psum.tile([P, C], F32, name="acc")
                 banks.append(acc)
-                for a in range(2):
-                    nc.tensor.matmul_mx(
-                        out=acc[:],
-                        lhsT=w4_t[:, 2 * e + a, 2 * P * h : 2 * P * h + 2 * P].bitcast(FP4X4),
-                        lhsT_scale=w4s_t[:, 2 * e + a, P * h : P * h + P],
-                        rhs=gcodes[2 + a][:, slots].bitcast(FP8X4),
-                        rhs_scale=gplanes[a][:, slots],
-                        start=(a == 0),
-                        stop=False,
-                    )
+                for g in (2, 0, 1):
+                    multiply(acc, h, e, g, g == 2, False)
             for e in range(E):
-                slots = slice(C * e, C * e + C)
-                for a in range(2):
-                    nc.tensor.matmul_mx(
-                        out=banks[e][:],
-                        lhsT=w8_t[h][:, 2 * e + a, :].bitcast(FP8X4),
-                        lhsT_scale=w8s_t[:, 2 * e + a, P * h : P * h + P],
-                        rhs=gcodes[a][:, slots].bitcast(FP8X4),
-                        rhs_scale=gplanes[a][4:P, slots],
-                        start=False,
-                        stop=(a == 1),
-                    )
-                nc.scalar.activation(y_t[h][:, slots], banks[e][:], SILU, bias=bias_t[:, h, e : e + 1])
+                multiply(banks[e], h, e, 3, False, True)
+                nc.scalar.activation(
+                    y_t[h][:, C * e : C * e + C], banks[e][:], SILU, bias=bias_t[:, h, e : e + 1]
+                )
 
-        for h in range(2):
-            first = keep.tile([P, T], F32, name=f"first{h}")
-            second = keep.tile([P, T], F32, name=f"second{h}")
-            result = keep.tile([P, T], F32, name=f"result{h}")
-            nc.vector.tensor_tensor(first[:], y_t[h][:].indirect(pos1_t[:]), gate_t[0][:], MULT)
-            nc.vector.tensor_tensor(second[:], y_t[h][:].indirect(pos2_t[:]), gate_t[1][:], MULT)
-            nc.vector.tensor_tensor(result[:], first[:], second[:], ADD)
-            nc.sync.dma_start(out[P * h : P * h + P, :], result[:])
+        half = T // 2
+        first = [keep.tile([P, T], F32, name=f"first{h}") for h in range(2)]
+        second = [keep.tile([P, T], F32, name=f"second{h}") for h in range(2)]
+        result = [keep.tile([P, T], F32, name=f"result{h}") for h in range(2)]
+
+        def fetch(dst, h, pos, i, cols):
+            nc.vector.tensor_tensor(
+                dst[h][:, cols],
+                y_t[h][:].indirect(pos[:, cols.start // 16 : cols.stop // 16]),
+                gate_t[:, i, cols],
+                MULT,
+            )
+
+        def finish(h, cols):
+            nc.vector.tensor_tensor(result[h][:, cols], first[h][:, cols], second[h][:, cols], ADD)
+            nc.sync.dma_start(out[P * h : P * h + P, cols], result[h][:, cols])
+
+        whole, left, right = slice(0, T), slice(0, half), slice(half, T)
+        fetch(first, 0, pos1_t, 0, whole)
+        fetch(second, 0, pos2_t, 1, whole)
+        fetch(first, 1, pos1_t, 0, whole)
+        finish(0, whole)
+        fetch(second, 1, pos2_t, 1, left)
+        fetch(second, 1, pos2_t, 1, right)
+        finish(1, left)
+        finish(1, right)

@@ -22,10 +22,11 @@ SILU = mybir.ActivationFunctionType.Silu
 MULT = mybir.AluOpType.mult
 ADD = mybir.AluOpType.add
 
-ORDER = ((0, 4), (2, 0), (1, 8), (3, 12))
+ORDER = ((0, 0, 4), (2, 0, 0), (1, 0, 8), (3, 1, 0))
 CHUNKS = {0: (256, 256, 256), 2: (512, 256), 1: (512, 256), 3: (512, 256)}
-LOADS = {0: (512, 256), 2: (512, 256), 1: (512, 256), 3: (512, 256)}
-ON_VECTOR = ((0, 1), (0, 2), (2, 1))
+LOADS = {0: (512, 256), 2: (512, 256), 1: (768,), 3: (512, 256)}
+WINDOW = 1376
+ON_VECTOR = ((0, 1), (0, 2))
 
 
 def tile_moe_cap2_lin_silu_kernel(
@@ -48,10 +49,9 @@ def tile_moe_cap2_lin_silu_kernel(
         bias_t = keep.tile([P, 2, E], F32, name="bias_t")
         gate_t = keep.tile([P, 2, T], F32, name="gate_t")
         y_t = [keep.tile([P, S + PAD], F32, name=f"y_t{h}") for h in range(2)]
-        planes = keep.tile([P, T], U8, name="planes", align_bytes=64)
-        gplanes = keep.tile([P, S], U8, name="gplanes", align_bytes=64)
-        moved = keep.tile([P, S], U8, name="moved", align_bytes=64)
-        codes = [keep.tile([P, T], U32, name=f"codes{g}", align_bytes=64) for g in range(4)]
+        planes = [keep.tile([P, w], U8, name=f"planes{i}", align_bytes=64) for i, w in enumerate((WINDOW, T))]
+        gplanes = [keep.tile([P, S], U8, name=f"gplanes{i}", align_bytes=64) for i in range(2)]
+        codes = [keep.tile([P, w], I32, name=f"codes{g}", align_bytes=64) for g, w in enumerate((WINDOW, WINDOW, WINDOW, T))]
         gcodes = [keep.tile([P, S], U32, name=f"gcodes{g}", align_bytes=64) for g in range(4)]
 
         warm = keep.tile([P, 8], F32, name="warm")
@@ -59,16 +59,18 @@ def tile_moe_cap2_lin_silu_kernel(
         warm2 = keep.tile([P, 8], F32, name="warm2")
         nc.scalar.activation(warm2[:], warm[:], SILU)
 
-        nc.gpsimd.memset(planes[:].bitcast(I32), 0)
-        nc.gpsimd.memset(moved[:].bitcast(I32), 0)
+        for i in range(2):
+            nc.gpsimd.memset(planes[i][:].bitcast(I32), 0)
+        for g in range(3):
+            nc.vector.memset(codes[g][:, T:WINDOW], 0)
         for t in (w8s_t, w4s_t):
-            nc.vector.memset(t[:].rearrange("p a n -> p (a n)").bitcast(I32), 0)
+            nc.gpsimd.memset(t[:].rearrange("p a n -> p (a n)").bitcast(I32), 0)
         for h in range(2):
             nc.vector.memset(y_t[h][:, S : S + PAD], 0.0)
 
-        nc.sync.dma_start(offs_t[:], offs)
         raw = {}
-        for g, _ in ORDER:
+
+        def load_x(g):
             rows = xT[512 * g : 512 * (g + 1), :].rearrange("(p j) w -> p j w", j=PACK)
             c0 = 0
             for w in LOADS[g]:
@@ -76,11 +78,17 @@ def tile_moe_cap2_lin_silu_kernel(
                 nc.sync.dma_start(r[:], rows[:, :, c0 : c0 + w])
                 raw[g, c0] = r
                 c0 += w
-        nc.gpsimd.dma_start(bias_t[:], b.rearrange("(h p) e -> p h e", h=2))
+
+        load_x(0)
+        nc.sync.dma_start(offs_t[:], offs)
+        load_x(2)
+        load_x(1)
+        load_x(3)
+        nc.sync.dma_start(bias_t[:], b.rearrange("(h p) e -> p h e", h=2))
         for dram, t in ((w4_scales, w4s_t), (w8_scales, w8s_t)):
             v = dram.rearrange("e a q n -> q (e a) n")
             for q in range(4):
-                nc.gpsimd.dma_start(
+                nc.sync.dma_start(
                     t[32 * q : 32 * q + 4, :, :].bitcast(I32), v[4 * q : 4 * q + 4, :, :].bitcast(I32)
                 )
         w4_v = w4_words.rearrange("e a p m -> p (e a) m")
@@ -95,19 +103,18 @@ def tile_moe_cap2_lin_silu_kernel(
                     w8_t[h][:, s, :].bitcast(I32), w8_v[:, s, 512 * h : 512 * h + 512].bitcast(I32)
                 )
 
-        load_w8(0, 2)
+        load_w8(0, 4)
         nc.sync.dma_start(pos1_t[:], pos1)
         nc.sync.dma_start(pos2_t[:], pos2)
-        nc.sync.dma_start(gate_t[:], gate[:, 0:P, :].rearrange("i p t -> p i t"))
-        load_w8(1, 2)
+        nc.sync.dma_start(gate_t[:, 0, :], gate[0, 0:P, :])
+        nc.sync.dma_start(gate_t[:, 1, :], gate[1, 0:P, :])
+        load_w8(1, 4)
 
         def gather(dst, table, pieces):
-            j = 0
-            for n in pieces:
-                nc.vector.tensor_copy(dst[:, j : j + n], table[:].indirect(offs_t[:, j // 16 : (j + n) // 16]))
-                j += n
+            for lo, hi in pieces:
+                nc.vector.tensor_copy(dst[:, lo:hi], table.indirect(offs_t[:, lo // 16 : hi // 16]))
 
-        for k, (g, row) in enumerate(ORDER):
+        for k, (g, i, row) in enumerate(ORDER):
             c0 = 0
             for ci, w in enumerate(CHUNKS[g]):
                 base = max(c for (gg, c) in raw if gg == g and c <= c0)
@@ -120,17 +127,21 @@ def tile_moe_cap2_lin_silu_kernel(
                     nc.scalar.copy(dst, src)
                 nc.vector.quantize_mx(
                     out=codes[g][:, c0 : c0 + w].bitcast(FP8X4),
-                    scales=planes[row:P, c0 : c0 + w],
+                    scales=planes[i][row:P, c0 : c0 + w],
                     in_=grouped[:].rearrange("p w t -> p (w t)"),
                 )
                 c0 += w
-            if k == 3:
-                gather(gplanes, planes, (512, 512))
-                for q in range(0, P, 32):
-                    nc.scalar.dma_start(
-                        moved[q : q + 4, :].bitcast(I32), gplanes[q + row : q + row + 4, :].bitcast(I32)
-                    )
-            gather(gcodes[g], codes[g], (512, 384, 128) if k == 3 else (512, 512))
+            if k == 2:
+                gather(gplanes[0], planes[0][:], ((0, 1024),))
+            if k < 3:
+                gather(gcodes[g], codes[g][:].bitcast(U32), ((0, 1024),))
+            else:
+                gather(gplanes[1], planes[1][:], ((0, 512),))
+                gather(gcodes[g], codes[g][:].bitcast(U32), ((0, 512),))
+                gather(gplanes[1], planes[1][:], ((512, 1024),))
+                gather(gcodes[g], codes[g][:].bitcast(U32), ((512, 768), (768, 896), (896, 1024)))
+
+        plane_of = {g: (gplanes[i], row) for g, i, row in ORDER}
 
         def multiply(acc, h, e, g, start, stop):
             slots = slice(C * e, C * e + C)
@@ -139,8 +150,7 @@ def tile_moe_cap2_lin_silu_kernel(
                 w, ws = w8_t[h][:, 2 * e + a, :].bitcast(FP8X4), w8s_t
             else:
                 w, ws = w4_t[:, 2 * e + a, 2 * P * h : 2 * P * h + 2 * P].bitcast(FP4X4), w4s_t
-            plane = moved if g == 3 else gplanes
-            row = 0 if g == 3 else dict(ORDER)[g]
+            plane, row = plane_of[g]
             nc.tensor.matmul_mx(
                 out=acc[:],
                 lhsT=w,
@@ -156,8 +166,10 @@ def tile_moe_cap2_lin_silu_kernel(
             for e in range(E):
                 acc = psum.tile([P, C], F32, name="acc")
                 banks.append(acc)
-                for g in (2, 0, 1):
-                    multiply(acc, h, e, g, g == 2, False)
+                multiply(acc, h, e, 2, True, False)
+            for e in range(E):
+                multiply(banks[e], h, e, 0, False, False)
+                multiply(banks[e], h, e, 1, False, False)
             for e in range(E):
                 multiply(banks[e], h, e, 3, False, True)
                 nc.scalar.activation(

from contextlib import ExitStack

import concourse.mybir as mybir

K, T, E, C, N = 2048, 768, 8, 128, 256
S = E * C
PAD = 32
P = 128
PACK = 4
FLOPS = 2 * K * S * N
BYTES = 4 * K * T + 3 * E * K * N // 4 + 2 * E * K * N // 64 + 4 * N * E + 4 * 2 * P * T + 2 * P * (S + 2 * T) // 16 + 4 * N * T

F32 = mybir.dt.float32
BF16 = mybir.dt.bfloat16
U32 = mybir.dt.uint32
I32 = mybir.dt.int32
U16 = mybir.dt.uint16
U8 = mybir.dt.uint8
FP8X4 = mybir.dt.float8_e4m3fn_x4
FP4X4 = mybir.dt.float4_e2m1fn_x4
SILU = mybir.ActivationFunctionType.Silu
MULT = mybir.AluOpType.mult
ADD = mybir.AluOpType.add

ORDER = ((0, 0, 4), (2, 0, 0), (1, 0, 8), (3, 1, 0))
CHUNKS = {0: (256, 256, 256), 2: (512, 256), 1: (512, 256), 3: (512, 256)}
LOADS = {0: (512, 256), 2: (512, 256), 1: (768,), 3: (512, 256)}
WINDOW = 1376
ON_VECTOR = ((0, 1), (0, 2))


def tile_moe_cap2_lin_silu_kernel(
    tc, xT, w8_words, w8_scales, w4_words, w4_scales, b, gate, offs, pos1, pos2, out
):
    nc = tc.nc
    with ExitStack() as ctx:
        lists = ctx.enter_context(tc.tile_pool(name="lists", bufs=1))
        keep = ctx.enter_context(tc.tile_pool(name="keep", bufs=1))
        psum = ctx.enter_context(tc.psum_pool(name="psum", bufs=8))

        offs_t = lists.tile([P, S // 16], U16, name="offs_t")
        pos1_t = lists.tile([P, T // 16], U16, name="pos1_t")
        pos2_t = lists.tile([P, T // 16], U16, name="pos2_t")

        w4_t = keep.tile([P, 2 * E, 2 * N], U8, name="w4_t", align_bytes=64)
        w8_t = [keep.tile([P, 2 * E, 4 * P], U8, name=f"w8_t{h}", align_bytes=64) for h in range(2)]
        w8s_t = keep.tile([P, 2 * E, N], U8, name="w8s_t", align_bytes=64)
        w4s_t = keep.tile([P, 2 * E, N], U8, name="w4s_t", align_bytes=64)
        bias_t = keep.tile([P, 2, E], F32, name="bias_t")
        gate_t = keep.tile([P, 2, T], F32, name="gate_t")
        y_t = [keep.tile([P, S + PAD], F32, name=f"y_t{h}") for h in range(2)]
        planes = [keep.tile([P, w], U8, name=f"planes{i}", align_bytes=64) for i, w in enumerate((WINDOW, T))]
        gplanes = [keep.tile([P, S], U8, name=f"gplanes{i}", align_bytes=64) for i in range(2)]
        codes = [keep.tile([P, w], I32, name=f"codes{g}", align_bytes=64) for g, w in enumerate((WINDOW, WINDOW, WINDOW, T))]
        gcodes = [keep.tile([P, S], U32, name=f"gcodes{g}", align_bytes=64) for g in range(4)]

        warm = keep.tile([P, 8], F32, name="warm")
        nc.vector.memset(warm[:], 0.0)
        warm2 = keep.tile([P, 8], F32, name="warm2")
        nc.scalar.activation(warm2[:], warm[:], SILU)

        for i in range(2):
            nc.gpsimd.memset(planes[i][:].bitcast(I32), 0)
        for g in range(3):
            nc.vector.memset(codes[g][:, T:WINDOW], 0)
        for t in (w8s_t, w4s_t):
            nc.gpsimd.memset(t[:].rearrange("p a n -> p (a n)").bitcast(I32), 0)
        for h in range(2):
            nc.vector.memset(y_t[h][:, S : S + PAD], 0.0)

        raw = {}

        def load_x(g):
            rows = xT[512 * g : 512 * (g + 1), :].rearrange("(p j) w -> p j w", j=PACK)
            c0 = 0
            for w in LOADS[g]:
                r = keep.tile([P, PACK, w], F32, name=f"raw{g}_{c0}")
                nc.sync.dma_start(r[:], rows[:, :, c0 : c0 + w])
                raw[g, c0] = r
                c0 += w

        load_x(0)
        nc.sync.dma_start(offs_t[:], offs)
        load_x(2)
        load_x(1)
        load_x(3)
        nc.sync.dma_start(bias_t[:], b.rearrange("(h p) e -> p h e", h=2))
        for dram, t in ((w4_scales, w4s_t), (w8_scales, w8s_t)):
            v = dram.rearrange("e a q n -> q (e a) n")
            for q in range(4):
                nc.sync.dma_start(
                    t[32 * q : 32 * q + 4, :, :].bitcast(I32), v[4 * q : 4 * q + 4, :, :].bitcast(I32)
                )
        w4_v = w4_words.rearrange("e a p m -> p (e a) m")
        nc.sync.dma_start(w4_t[:].bitcast(I32), w4_v.bitcast(I32))
        w8_v = w8_words.rearrange("e a p n r -> p (e a) (n r)")

        def load_w8(h, parts):
            n = 16 // parts
            for i in range(parts):
                s = slice(n * i, n * i + n)
                nc.sync.dma_start(
                    w8_t[h][:, s, :].bitcast(I32), w8_v[:, s, 512 * h : 512 * h + 512].bitcast(I32)
                )

        load_w8(0, 4)
        nc.sync.dma_start(pos1_t[:], pos1)
        nc.sync.dma_start(pos2_t[:], pos2)
        nc.sync.dma_start(gate_t[:, 0, :], gate[0, 0:P, :])
        nc.sync.dma_start(gate_t[:, 1, :], gate[1, 0:P, :])
        load_w8(1, 4)

        def gather(dst, table, pieces):
            for lo, hi in pieces:
                nc.vector.tensor_copy(dst[:, lo:hi], table.indirect(offs_t[:, lo // 16 : hi // 16]))

        for k, (g, i, row) in enumerate(ORDER):
            c0 = 0
            for ci, w in enumerate(CHUNKS[g]):
                base = max(c for (gg, c) in raw if gg == g and c <= c0)
                src = raw[g, base][:, :, c0 - base : c0 - base + w].rearrange("p t (c i) -> p c t i", i=4)
                grouped = keep.tile([P, w, PACK], BF16, name=f"grouped{g}_{c0}", align_bytes=64)
                dst = grouped[:].rearrange("p (c i) t -> p c t i", i=4)
                if (g, ci) in ON_VECTOR:
                    nc.vector.tensor_copy(dst, src)
                else:
                    nc.scalar.copy(dst, src)
                nc.vector.quantize_mx(
                    out=codes[g][:, c0 : c0 + w].bitcast(FP8X4),
                    scales=planes[i][row:P, c0 : c0 + w],
                    in_=grouped[:].rearrange("p w t -> p (w t)"),
                )
                c0 += w
            if k == 2:
                gather(gplanes[0], planes[0][:], ((0, 1024),))
            if k < 3:
                gather(gcodes[g], codes[g][:].bitcast(U32), ((0, 1024),))
            else:
                gather(gplanes[1], planes[1][:], ((0, 512),))
                gather(gcodes[g], codes[g][:].bitcast(U32), ((0, 512),))
                gather(gplanes[1], planes[1][:], ((512, 1024),))
                gather(gcodes[g], codes[g][:].bitcast(U32), ((512, 768), (768, 896), (896, 1024)))

        plane_of = {g: (gplanes[i], row) for g, i, row in ORDER}

        def multiply(acc, h, e, g, start, stop):
            slots = slice(C * e, C * e + C)
            a = g % 2
            if g < 2:
                w, ws = w8_t[h][:, 2 * e + a, :].bitcast(FP8X4), w8s_t
            else:
                w, ws = w4_t[:, 2 * e + a, 2 * P * h : 2 * P * h + 2 * P].bitcast(FP4X4), w4s_t
            plane, row = plane_of[g]
            nc.tensor.matmul_mx(
                out=acc[:],
                lhsT=w,
                lhsT_scale=ws[:, 2 * e + a, P * h : P * h + P],
                rhs=gcodes[g][:, slots].bitcast(FP8X4),
                rhs_scale=plane[row:P, slots],
                start=start,
                stop=stop,
            )

        for h in range(2):
            banks = []
            for e in range(E):
                acc = psum.tile([P, C], F32, name="acc")
                banks.append(acc)
                multiply(acc, h, e, 2, True, False)
            for e in range(E):
                multiply(banks[e], h, e, 0, False, False)
                multiply(banks[e], h, e, 1, False, False)
            for e in range(E):
                multiply(banks[e], h, e, 3, False, True)
                nc.scalar.activation(
                    y_t[h][:, C * e : C * e + C], banks[e][:], SILU, bias=bias_t[:, h, e : e + 1]
                )

        half = T // 2
        first = [keep.tile([P, T], F32, name=f"first{h}") for h in range(2)]
        second = [keep.tile([P, T], F32, name=f"second{h}") for h in range(2)]
        result = [keep.tile([P, T], F32, name=f"result{h}") for h in range(2)]

        def fetch(dst, h, pos, i, cols):
            nc.vector.tensor_tensor(
                dst[h][:, cols],
                y_t[h][:].indirect(pos[:, cols.start // 16 : cols.stop // 16]),
                gate_t[:, i, cols],
                MULT,
            )

        def finish(h, cols):
            nc.vector.tensor_tensor(result[h][:, cols], first[h][:, cols], second[h][:, cols], ADD)
            nc.sync.dma_start(out[P * h : P * h + P, cols], result[h][:, cols])

        whole, left, right = slice(0, T), slice(0, half), slice(half, T)
        fetch(first, 0, pos1_t, 0, whole)
        fetch(second, 0, pos2_t, 1, whole)
        fetch(first, 1, pos1_t, 0, whole)
        finish(0, whole)
        fetch(second, 1, pos2_t, 1, left)
        fetch(second, 1, pos2_t, 1, right)
        finish(1, left)
        finish(1, right)
